import numpy as np
import ml_dtypes


def mxq(x, axis, fmt="e4m3"):
    dtype, down = {"e4m3": (ml_dtypes.float8_e4m3fn, 7), "e5m2": (ml_dtypes.float8_e5m2, 14)}[fmt]
    v = np.moveaxis(np.asarray(x, np.float32).astype(ml_dtypes.bfloat16).astype(np.float64), axis, -1)
    blocks = v.reshape(v.shape[:-1] + (-1, 32))
    amax = np.abs(blocks).max(-1, keepdims=True)
    byte = np.maximum(np.where(amax > 0, np.frexp(amax)[1] - 1 + 127, 0) - down, 1)
    scale = np.exp2(byte - 127.0)
    codes = (blocks / scale).astype(np.float32).astype(dtype).astype(np.float64)
    return np.moveaxis((codes * scale).reshape(v.shape), -1, axis)


WIDE = False


def mx_kscale(k):
    if not WIDE:
        return np.ones(k)
    levels = np.array([10, -10, 5, -5, 0])
    if k % 512:
        return np.exp2(np.random.permutation(np.resize(levels, k // 32))).repeat(32)
    a = np.empty((k // 512, 16))
    for p in range(k // 512):
        a[p, :8] = np.random.permutation(np.resize(levels, 8))
        for g in range(8):
            far = levels[np.abs(levels - a[p, g]) >= 10]
            a[p, g + 8] = far[np.random.randint(len(far))]
    return np.exp2(a.ravel()).repeat(32)


def f64(x):
    return np.asarray(x).astype(np.float64)


def striped(idx):
    return np.tile(np.asarray(idx).reshape(-1, 16).T, (8, 1)).astype(np.uint16)


def unstriped(offs):
    return offs[:16].T.reshape(-1).astype(np.int64)


E2M1 = np.array([0.0, 0.5, 1.0, 1.5, 2.0, 3.0, 4.0, 6.0, -0.0, -0.5, -1.0, -1.5, -2.0, -3.0, -4.0, -6.0])


def pack_weight(w, fmt):
    k, n = w.shape
    w = f64(np.asarray(w, np.float32).astype(ml_dtypes.bfloat16)).reshape(k // 32, 32, n)
    amax = np.abs(w).max(1)
    if fmt == "e4m3":
        byte = np.frexp(amax)[1] - 1 + 127 - 7
    else:
        mant, ex = np.frexp(amax / 6.0)
        byte = np.where(mant > 0.5, ex, ex - 1) + 127
    byte = np.clip(np.where(amax > 0, byte, 1), 1, 254)
    scaled = (w * np.exp2(127.0 - byte)[:, None, :]).reshape(k, n).astype(np.float32)
    by_word = np.ascontiguousarray(scaled.reshape(k // 512, 128, 4, n).transpose(0, 1, 3, 2))
    if fmt == "e4m3":
        words = by_word.astype(ml_dtypes.float8_e4m3fn).view(np.uint8)
    else:
        c = by_word.astype(ml_dtypes.float4_e2m1fn).view(np.uint8) & 0xF
        words = (c[..., 0::2] | (c[..., 1::2] << 4)).reshape(k // 512, 128, 2 * n)
    return np.ascontiguousarray(words), np.ascontiguousarray(byte.astype(np.uint8).reshape(k // 512, 16, n))


def unpack_weight(words, scales, fmt):
    g, _, n = scales.shape
    words = np.ascontiguousarray(words).reshape(g, 128, n, -1)
    if fmt == "e4m3":
        vals = words.view(ml_dtypes.float8_e4m3fn).astype(np.float64)
    else:
        nib = np.empty((g, 128, n, 4), np.uint8)
        nib[..., 0::2] = words & 0xF
        nib[..., 1::2] = words >> 4
        vals = E2M1[nib]
    vals = vals * np.repeat(np.exp2(scales.astype(np.float64) - 127.0), 8, axis=1)[..., None]
    return vals.transpose(0, 1, 3, 2).reshape(g * 512, n)


D, T, I, G, U, Q, E = 512, 4096, 2048, 512, 2048, 128, 512


def setup_inputs():
    n = np.random.standard_normal
    idx = np.random.permutation(T)[:I]
    idx2 = np.random.permutation(U)[:G]
    fd = mx_kscale(D)
    fg = mx_kscale(G)
    tg = np.ones(U)
    tg[idx2] = fg
    keysp = pack_weight(n((D, T)) / fd[:, None], "e4m3")
    return {
        "query": (n((D, Q)) * 0.2 / np.sqrt(D) * fd[:, None]).astype(np.float32),
        "keys_words": keysp[0],
        "keys_scales": keysp[1],
        "size": (np.random.uniform(0.5, 2.0, (1, G)) * fg).astype(np.float32),
        "vals": (n((E, U)) / tg).astype(np.float32),
        "offs": striped(idx),
        "offs2": striped(idx2),
    }


def reference(query, keys_words, keys_scales, size, vals, offs, offs2):
    idx = unstriped(offs)
    idx2 = unstriped(offs2)
    keysu = unpack_weight(keys_words, keys_scales, "e4m3")
    queryq = mxq(f64(query), 0, "e4m3")
    keysidxg = keysu[:, idx]
    a = queryq.T @ keysidxg
    s = a.reshape(Q, G, I // G).max(axis=2)
    p = np.exp(s - np.max(s, axis=1, keepdims=True))
    w = p * f64(size) / np.sum(p, axis=1, keepdims=True)
    wt = w.T
    vt = f64(vals)[:, idx2].T
    wtq = mxq(wt, 0, "e4m3")
    vtq = mxq(vt, 0, "e4m3")
    o = wtq.T @ vtq
    return o

@@ -1,0 +1,176 @@
+from contextlib import ExitStack
+
+import concourse.mybir as mybir
+from concourse.masks import make_identity
+
+D, T, I, G, U, Q, E = 512, 4096, 2048, 512, 2048, 128, 512
+FLOPS = 2 * D * Q * I + 2 * G * Q * E
+
+F32 = mybir.dt.float32
+BF16 = mybir.dt.bfloat16
+I32 = mybir.dt.int32
+U32 = mybir.dt.uint32
+U16 = mybir.dt.uint16
+U8 = mybir.dt.uint8
+FP8X4 = mybir.dt.float8_e4m3fn_x4
+ACT = mybir.ActivationFunctionType
+ALU = mybir.AluOpType
+AXIS_X = mybir.AxisListType.X
+
+P = 128
+PACK = 4
+CHUNK = 512
+SCALAR_BLOCKS = 2
+CAST_PIECES = 2
+
+
+def tile_attend_wordmax_kernel(tc, query, keys_words, keys_scales, size, vals, offs, offs2, out):
+    nc = tc.nc
+    with ExitStack() as ctx:
+        keep = ctx.enter_context(tc.tile_pool(name="keep", bufs=1))
+        psum = ctx.enter_context(tc.psum_pool(name="psum", bufs=1))
+
+        token_list = keep.tile([P, I // 16], U16, name="token_list")
+        nc.sync.dma_start(token_list[:], offs)
+        scale_pool = keep.tile([P, T], U8, name="scale_pool", align_bytes=64)
+        nc.vector.memset(scale_pool[:].bitcast(I32), 0)
+        for r in range(4):
+            nc.scalar.dma_start(scale_pool[r:P:32, :].bitcast(I32), keys_scales[0, r:16:4, :].bitcast(I32))
+        q_raw = keep.tile([P, PACK, Q], F32, name="q_raw")
+        nc.sync.dma_start(q_raw[:], query.rearrange("(p j) q -> p j q", j=PACK))
+        word_pool = keep.tile([P, T], I32, name="word_pool", align_bytes=64)
+        nc.sync.dma_start(word_pool[:], keys_words[0].rearrange("p n t -> p (n t)").bitcast(I32))
+        word_list = keep.tile([P, G // 16], U16, name="word_list")
+        nc.sync.dma_start(word_list[:], offs2)
+        size_cols = keep.tile([P, PACK], F32, name="size_cols")
+        nc.sync.dma_start(size_cols[:], size.rearrange("o (p t) -> p (o t)", t=PACK))
+        v_raw = []
+        for b in range(E // P):
+            raw = keep.tile([P, U], F32, name="v_raw%d" % b)
+            pieces = CAST_PIECES if b < SCALAR_BLOCKS else 1
+            for h in range(pieces):
+                cols = slice(h * U // pieces, (h + 1) * U // pieces)
+                nc.sync.dma_start(raw[:, cols], vals[b * P : (b + 1) * P, cols])
+            v_raw.append(raw)
+
+        ident = keep.tile([P, P], F32, name="ident")
+        make_identity(nc, ident[:])
+        warm = keep.tile([P, 1], F32, name="warm")
+        nc.scalar.activation(warm[:], ident[:, 0:1], ACT.Exp)
+
+        q_bf = keep.tile([P, Q * PACK], BF16, name="q_bf", align_bytes=64)
+        nc.vector.tensor_copy(q_bf[:].rearrange("p (q j) -> p q j", j=PACK), q_raw[:].rearrange("p j q -> p q j"))
+        q_codes = keep.tile([P, Q], U32, name="q_codes", align_bytes=64)
+        q_scales = keep.tile([P, Q], U8, name="q_scales", align_bytes=64)
+        nc.vector.quantize_mx(out=q_codes[:].bitcast(FP8X4), scales=q_scales[:], in_=q_bf[:])
+
+        size_bank = psum.tile([P, PACK, P], F32, name="size_bank")
+        for t in range(PACK):
+            nc.tensor.transpose(size_bank[:, t, :], size_cols[:, t : t + 1].to_broadcast([P, P]), ident[:])
+
+        v_codes = keep.tile([P, E], U32, name="v_codes", align_bytes=64)
+        v_scales = keep.tile([P, E], U8, name="v_scales", align_bytes=64)
+        v_turned = []
+
+        def gather_values(b):
+            picked = keep.tile([P, G], BF16, name="v_picked%d" % b, align_bytes=64)
+            if b < SCALAR_BLOCKS:
+                window = keep.tile([P, U], BF16, name="v_window%d" % b, align_bytes=64)
+                for h in range(CAST_PIECES):
+                    cols = slice(h * U // CAST_PIECES, (h + 1) * U // CAST_PIECES)
+                    nc.scalar.activation(window[:, cols], v_raw[b][:, cols], ACT.Copy)
+                nc.scalar.activation(picked[:], window[:].indirect(word_list[:]), ACT.Copy)
+            else:
+                nc.vector.tensor_copy(picked[:], v_raw[b][:].indirect(word_list[:]))
+            pairs = picked[:].bitcast(F32)
+            bank = psum.tile([P, 2, P], F32, name="v_bank", tag="v_bank", bufs=2)
+            for u in range(2):
+                nc.tensor.transpose(bank[:, u, :], pairs[:, u : G // 2 : 2], ident[:])
+            turned = keep.tile([P, P * PACK], BF16, name="v_turned%d" % b, align_bytes=64)
+            nc.scalar.copy(turned[:].bitcast(F32).rearrange("p (e u) -> p e u", u=2), bank[:].rearrange("p u e -> p e u"))
+            v_turned.append(turned)
+
+        def quantize_values(b):
+            cols = slice(b * P, (b + 1) * P)
+            nc.vector.quantize_mx(out=v_codes[:, cols].bitcast(FP8X4), scales=v_scales[:, cols], in_=v_turned[b][:])
+
+        key_scales = keep.tile([P, I], U8, name="key_scales", align_bytes=64)
+        nc.vector.tensor_copy(key_scales[:], scale_pool[:].indirect(token_list[:]))
+        s = keep.tile([P, G], F32, name="s")
+        banks = []
+
+        def score(c):
+            key_codes = keep.tile([P, CHUNK], U32, name="key_codes%d" % c, align_bytes=64)
+            slots = token_list[:, c * CHUNK // 16 : (c + 1) * CHUNK // 16]
+            nc.vector.tensor_copy(key_codes[:], word_pool[:].bitcast(U32).indirect(slots))
+            bank = psum.tile([P, CHUNK], F32, name="acc", tag="acc", bufs=4)
+            nc.tensor.matmul_mx(
+                out=bank[:],
+                lhsT=q_codes[:].bitcast(FP8X4),
+                lhsT_scale=q_scales[:],
+                rhs=key_codes[:].bitcast(FP8X4),
+                rhs_scale=key_scales[:, c * CHUNK : (c + 1) * CHUNK],
+                start=True,
+                stop=True,
+            )
+            banks.append(bank)
+
+        def best_token(c):
+            words = slice(c * CHUNK // PACK, (c + 1) * CHUNK // PACK)
+            nc.vector.tensor_reduce(s[:, words], banks[c][:].rearrange("q (g r) -> q g r", r=PACK), AXIS_X, ALU.max)
+
+        for b in range(SCALAR_BLOCKS):
+            gather_values(b)
+        chunks = I // CHUNK
+        for c in range(chunks):
+            score(c)
+            if c > 0:
+                best_token(c - 1)
+        best_token(chunks - 1)
+
+        neg_max = keep.tile([P, 1], F32, name="neg_max")
+        nc.vector.tensor_reduce(neg_max[:], s[:], AXIS_X, ALU.max, negate=True)
+        p = keep.tile([P, G], F32, name="p")
+        row_sum = keep.tile([P, 1], F32, name="row_sum")
+        nc.scalar.activation(p[:], s[:], ACT.Exp, bias=neg_max[:], scale=1.0, accum_out=row_sum[:])
+        for b in range(SCALAR_BLOCKS):
+            quantize_values(b)
+        inv_sum = keep.tile([P, 1], F32, name="inv_sum")
+        nc.vector.reciprocal(inv_sum[:], row_sum[:])
+        w = keep.tile([P, G], BF16, name="w", align_bytes=64)
+        nc.vector.scalar_tensor_tensor(
+            w[:].rearrange("q (p t) -> q p t", t=PACK),
+            p[:].rearrange("q (p t) -> q p t", t=PACK),
+            inv_sum[:],
+            size_bank[:].rearrange("q t p -> q p t"),
+            ALU.mult,
+            ALU.mult,
+        )
+        w_pairs = w[:].bitcast(F32)
+        w_bank = psum.tile([P, 2, P], F32, name="w_bank")
+        for u in range(2):
+            nc.tensor.transpose(w_bank[:, u, :], w_pairs[:, u : G // 2 : 2], ident[:])
+        w_turned = keep.tile([P, Q * PACK], BF16, name="w_turned", align_bytes=64)
+        nc.scalar.copy(w_turned[:].bitcast(F32).rearrange("p (q u) -> p q u", u=2), w_bank[:].rearrange("p u q -> p q u"))
+        for b in range(SCALAR_BLOCKS, E // P):
+            gather_values(b)
+        w_codes = keep.tile([P, Q], U32, name="w_codes", align_bytes=64)
+        w_scales = keep.tile([P, Q], U8, name="w_scales", align_bytes=64)
+        nc.vector.quantize_mx(out=w_codes[:].bitcast(FP8X4), scales=w_scales[:], in_=w_turned[:])
+        for b in range(SCALAR_BLOCKS, E // P):
+            quantize_values(b)
+
+        for part, (lo, hi) in enumerate(((0, 256), (256, 384), (384, 512))):
+            bank = psum.tile([P, hi - lo], F32, name="acc", tag="acc", bufs=4)
+            nc.tensor.matmul_mx(
+                out=bank[:],
+                lhsT=w_codes[:].bitcast(FP8X4),
+                lhsT_scale=w_scales[:],
+                rhs=v_codes[:, lo:hi].bitcast(FP8X4),
+                rhs_scale=v_scales[:, lo:hi],
+                start=True,
+                stop=True,
+            )
+            result = keep.tile([P, hi - lo], F32, name="result%d" % part)
+            nc.scalar.copy(result[:], bank[:])
+            nc.sync.dma_start(out[:, lo:hi], result[:])

@@ -20,8 +20,8 @@ AXIS_X = mybir.AxisListType.X
 P = 128
 PACK = 4
 CHUNK = 512
-SCALAR_BLOCKS = 2
-CAST_PIECES = 2
+PARTS = ((0, 256), (256, 512))
+CAST_PIECES = 4
 
 
 def tile_attend_wordmax_kernel(tc, query, keys_words, keys_scales, size, vals, offs, offs2, out):
@@ -30,77 +30,87 @@ def tile_attend_wordmax_kernel(tc, query, keys_words, keys_scales, size, vals, o
         keep = ctx.enter_context(tc.tile_pool(name="keep", bufs=1))
         psum = ctx.enter_context(tc.psum_pool(name="psum", bufs=1))
 
+        def shared(slot, shape, dtype, name):
+            return keep.tile(shape, dtype, name=name, tag=slot, align_bytes=64)
+
         token_list = keep.tile([P, I // 16], U16, name="token_list")
         nc.sync.dma_start(token_list[:], offs)
-        scale_pool = keep.tile([P, T], U8, name="scale_pool", align_bytes=64)
-        nc.vector.memset(scale_pool[:].bitcast(I32), 0)
-        for r in range(4):
-            nc.scalar.dma_start(scale_pool[r:P:32, :].bitcast(I32), keys_scales[0, r:16:4, :].bitcast(I32))
-        q_raw = keep.tile([P, PACK, Q], F32, name="q_raw")
+        q_raw = shared("slot_s", [P, PACK, Q], F32, "q_raw")
         nc.sync.dma_start(q_raw[:], query.rearrange("(p j) q -> p j q", j=PACK))
-        word_pool = keep.tile([P, T], I32, name="word_pool", align_bytes=64)
-        nc.sync.dma_start(word_pool[:], keys_words[0].rearrange("p n t -> p (n t)").bitcast(I32))
         word_list = keep.tile([P, G // 16], U16, name="word_list")
         nc.sync.dma_start(word_list[:], offs2)
-        size_cols = keep.tile([P, PACK], F32, name="size_cols")
-        nc.sync.dma_start(size_cols[:], size.rearrange("o (p t) -> p (o t)", t=PACK))
-        v_raw = []
-        for b in range(E // P):
-            raw = keep.tile([P, U], F32, name="v_raw%d" % b)
-            pieces = CAST_PIECES if b < SCALAR_BLOCKS else 1
-            for h in range(pieces):
-                cols = slice(h * U // pieces, (h + 1) * U // pieces)
-                nc.sync.dma_start(raw[:, cols], vals[b * P : (b + 1) * P, cols])
-            v_raw.append(raw)
+        scale_pool = shared("slot_c", [P, T], U8, "scale_pool")
+        nc.vector.memset(scale_pool[:].bitcast(I32), 0)
+        for r in range(4):
+            nc.sync.dma_start(scale_pool[r:P:32, :].bitcast(I32), keys_scales[0, r:16:4, :].bitcast(I32))
 
         ident = keep.tile([P, P], F32, name="ident")
         make_identity(nc, ident[:])
-        warm = keep.tile([P, 1], F32, name="warm")
-        nc.scalar.activation(warm[:], ident[:, 0:1], ACT.Exp)
+        zero = shared("slot_k", [P, 1], F32, "zero")
+        nc.vector.memset(zero[:], 0.0)
+        warm = shared("slot_a", [P, 1], F32, "warm")
+        nc.scalar.activation(warm[:], zero[:], ACT.Exp)
+        word_pool = shared("slot_k", [P, T], I32, "word_pool")
+        nc.sync.dma_start(word_pool[:], keys_words[0].rearrange("p n t -> p (n t)").bitcast(I32))
 
-        q_bf = keep.tile([P, Q * PACK], BF16, name="q_bf", align_bytes=64)
+
+        q_bf = shared("slot_b", [P, Q * PACK], BF16, "q_bf")
         nc.vector.tensor_copy(q_bf[:].rearrange("p (q j) -> p q j", j=PACK), q_raw[:].rearrange("p j q -> p q j"))
         q_codes = keep.tile([P, Q], U32, name="q_codes", align_bytes=64)
         q_scales = keep.tile([P, Q], U8, name="q_scales", align_bytes=64)
         nc.vector.quantize_mx(out=q_codes[:].bitcast(FP8X4), scales=q_scales[:], in_=q_bf[:])
 
+        size_cols = shared("slot_s", [P, PACK], F32, "size_cols")
+        nc.sync.dma_start(size_cols[:], size.rearrange("o (p t) -> p (o t)", t=PACK))
         size_bank = psum.tile([P, PACK, P], F32, name="size_bank")
         for t in range(PACK):
             nc.tensor.transpose(size_bank[:, t, :], size_cols[:, t : t + 1].to_broadcast([P, P]), ident[:])
 
-        v_codes = keep.tile([P, E], U32, name="v_codes", align_bytes=64)
-        v_scales = keep.tile([P, E], U8, name="v_scales", align_bytes=64)
-        v_turned = []
+        key_scales = keep.tile([P, I], U8, name="key_scales", align_bytes=64)
+        nc.vector.tensor_copy(key_scales[:], scale_pool[:].indirect(token_list[:]))
 
-        def gather_values(b):
-            picked = keep.tile([P, G], BF16, name="v_picked%d" % b, align_bytes=64)
-            if b < SCALAR_BLOCKS:
-                window = keep.tile([P, U], BF16, name="v_window%d" % b, align_bytes=64)
-                for h in range(CAST_PIECES):
-                    cols = slice(h * U // CAST_PIECES, (h + 1) * U // CAST_PIECES)
-                    nc.scalar.activation(window[:, cols], v_raw[b][:, cols], ACT.Copy)
-                nc.scalar.activation(picked[:], window[:].indirect(word_list[:]), ACT.Copy)
-            else:
-                nc.vector.tensor_copy(picked[:], v_raw[b][:].indirect(word_list[:]))
+        v_scales = keep.tile([P, E], U8, name="v_scales", align_bytes=64)
+        v_raw = []
+
+        def load_values(b):
+            raw = shared(("slot_a", "slot_b", "slot_c", "slot_d")[b], [P, U], F32, "v_raw%d" % b)
+            pieces = CAST_PIECES if b < 2 else 1
+            for h in range(pieces):
+                cols = slice(h * U // pieces, (h + 1) * U // pieces)
+                nc.sync.dma_start(raw[:, cols], vals[b * P : (b + 1) * P, cols])
+            v_raw.append(raw)
+
+        for b in range(3):
+            load_values(b)
+        v_turned = keep.tile([P, E * PACK], BF16, name="v_turned", align_bytes=64)
+
+        def turn_values(b, picked):
             pairs = picked[:].bitcast(F32)
             bank = psum.tile([P, 2, P], F32, name="v_bank", tag="v_bank", bufs=2)
             for u in range(2):
                 nc.tensor.transpose(bank[:, u, :], pairs[:, u : G // 2 : 2], ident[:])
-            turned = keep.tile([P, P * PACK], BF16, name="v_turned%d" % b, align_bytes=64)
-            nc.scalar.copy(turned[:].bitcast(F32).rearrange("p (e u) -> p e u", u=2), bank[:].rearrange("p u e -> p e u"))
-            v_turned.append(turned)
+            turned = v_turned[:, b * P * PACK : (b + 1) * P * PACK]
+            nc.scalar.copy(turned.bitcast(F32).rearrange("p (e u) -> p e u", u=2), bank[:].rearrange("p u e -> p e u"))
 
-        def quantize_values(b):
-            cols = slice(b * P, (b + 1) * P)
-            nc.vector.quantize_mx(out=v_codes[:, cols].bitcast(FP8X4), scales=v_scales[:, cols], in_=v_turned[b][:])
+        def gather_on_scalar(b):
+            window = shared("slot_w", [P, U], BF16, "v_window%d" % b)
+            for h in range(CAST_PIECES):
+                cols = slice(h * U // CAST_PIECES, (h + 1) * U // CAST_PIECES)
+                nc.scalar.activation(window[:, cols], v_raw[b][:, cols], ACT.Copy)
+            picked = keep.tile([P, G], BF16, name="v_picked%d" % b, align_bytes=64)
+            nc.scalar.activation(picked[:], window[:].indirect(word_list[:]), ACT.Copy)
+            turn_values(b, picked)
 
-        key_scales = keep.tile([P, I], U8, name="key_scales", align_bytes=64)
-        nc.vector.tensor_copy(key_scales[:], scale_pool[:].indirect(token_list[:]))
+        def gather_on_vector(b):
+            picked = keep.tile([P, G], BF16, name="v_picked%d" % b, align_bytes=64)
+            nc.vector.tensor_copy(picked[:], v_raw[b][:].indirect(word_list[:]))
+            turn_values(b, picked)
+
         s = keep.tile([P, G], F32, name="s")
         banks = []
 
         def score(c):
-            key_codes = keep.tile([P, CHUNK], U32, name="key_codes%d" % c, align_bytes=64)
+            key_codes = shared("slot_d" if c == 0 else "key_codes%d" % c, [P, CHUNK], U32, "key_codes%d" % c)
             slots = token_list[:, c * CHUNK // 16 : (c + 1) * CHUNK // 16]
             nc.vector.tensor_copy(key_codes[:], word_pool[:].bitcast(U32).indirect(slots))
             bank = psum.tile([P, CHUNK], F32, name="acc", tag="acc", bufs=4)
@@ -119,48 +129,50 @@ def tile_attend_wordmax_kernel(tc, query, keys_words, keys_scales, size, vals, o
             words = slice(c * CHUNK // PACK, (c + 1) * CHUNK // PACK)
             nc.vector.tensor_reduce(s[:, words], banks[c][:].rearrange("q (g r) -> q g r", r=PACK), AXIS_X, ALU.max)
 
-        for b in range(SCALAR_BLOCKS):
-            gather_values(b)
+        gather_on_scalar(0)
+        gather_on_scalar(1)
         chunks = I // CHUNK
         for c in range(chunks):
             score(c)
             if c > 0:
                 best_token(c - 1)
+            else:
+                load_values(3)
         best_token(chunks - 1)
 
         neg_max = keep.tile([P, 1], F32, name="neg_max")
         nc.vector.tensor_reduce(neg_max[:], s[:], AXIS_X, ALU.max, negate=True)
-        p = keep.tile([P, G], F32, name="p")
+        p = shared("slot_w", [P, G], F32, "p")
         row_sum = keep.tile([P, 1], F32, name="row_sum")
         nc.scalar.activation(p[:], s[:], ACT.Exp, bias=neg_max[:], scale=1.0, accum_out=row_sum[:])
-        for b in range(SCALAR_BLOCKS):
-            quantize_values(b)
-        inv_sum = keep.tile([P, 1], F32, name="inv_sum")
+        gather_on_vector(2)
+        gather_on_vector(3)
+        inv_sum = shared("slot_d", [P, 1], F32, "inv_sum")
         nc.vector.reciprocal(inv_sum[:], row_sum[:])
-        w = keep.tile([P, G], BF16, name="w", align_bytes=64)
-        nc.vector.scalar_tensor_tensor(
-            w[:].rearrange("q (p t) -> q p t", t=PACK),
-            p[:].rearrange("q (p t) -> q p t", t=PACK),
-            inv_sum[:],
-            size_bank[:].rearrange("q t p -> q p t"),
-            ALU.mult,
-            ALU.mult,
-        )
-        w_pairs = w[:].bitcast(F32)
         w_bank = psum.tile([P, 2, P], F32, name="w_bank")
         for u in range(2):
-            nc.tensor.transpose(w_bank[:, u, :], w_pairs[:, u : G // 2 : 2], ident[:])
+            w = keep.tile([P, P, 2], BF16, name="w%d" % u, align_bytes=64)
+            nc.vector.scalar_tensor_tensor(
+                w[:],
+                p[:].rearrange("q (p t) -> q p t", t=PACK)[:, :, 2 * u : 2 * u + 2],
+                inv_sum[:],
+                size_bank[:, 2 * u : 2 * u + 2, :].rearrange("q t p -> q p t"),
+                ALU.mult,
+                ALU.mult,
+            )
+            nc.tensor.transpose(w_bank[:, u, :], w[:].rearrange("q p t -> q (p t)").bitcast(F32), ident[:])
+        v_codes = shared("slot_w", [P, E], U32, "v_codes")
+        for lo, hi in ((0, 256), (256, 384), (384, 512)):
+            nc.vector.quantize_mx(
+                out=v_codes[:, lo:hi].bitcast(FP8X4), scales=v_scales[:, lo:hi], in_=v_turned[:, lo * PACK : hi * PACK]
+            )
         w_turned = keep.tile([P, Q * PACK], BF16, name="w_turned", align_bytes=64)
-        nc.scalar.copy(w_turned[:].bitcast(F32).rearrange("p (q u) -> p q u", u=2), w_bank[:].rearrange("p u q -> p q u"))
-        for b in range(SCALAR_BLOCKS, E // P):
-            gather_values(b)
+        nc.vector.tensor_copy(w_turned[:].bitcast(F32).rearrange("p (q u) -> p q u", u=2), w_bank[:].rearrange("p u q -> p q u"))
         w_codes = keep.tile([P, Q], U32, name="w_codes", align_bytes=64)
         w_scales = keep.tile([P, Q], U8, name="w_scales", align_bytes=64)
         nc.vector.quantize_mx(out=w_codes[:].bitcast(FP8X4), scales=w_scales[:], in_=w_turned[:])
-        for b in range(SCALAR_BLOCKS, E // P):
-            quantize_values(b)
 
-        for part, (lo, hi) in enumerate(((0, 256), (256, 384), (384, 512))):
+        for part, (lo, hi) in enumerate(PARTS):
             bank = psum.tile([P, hi - lo], F32, name="acc", tag="acc", bufs=4)
             nc.tensor.matmul_mx(
                 out=bank[:],
@@ -172,5 +184,8 @@ def tile_attend_wordmax_kernel(tc, query, keys_words, keys_scales, size, vals, o
                 stop=True,
             )
             result = keep.tile([P, hi - lo], F32, name="result%d" % part)
-            nc.scalar.copy(result[:], bank[:])
+            if part == len(PARTS) - 1:
+                nc.vector.tensor_copy(result[:], bank[:])
+            else:
+                nc.scalar.copy(result[:], bank[:])
             nc.sync.dma_start(out[:, lo:hi], result[:])

@@ -19,9 +19,10 @@ AXIS_X = mybir.AxisListType.X
 
 P = 128
 PACK = 4
+CAST_PIECES = 4
+PIECE = U // CAST_PIECES
 CHUNK = 512
 PARTS = ((0, 256), (256, 512))
-CAST_PIECES = 4
 
 
 def tile_attend_wordmax_kernel(tc, query, keys_words, keys_scales, size, vals, offs, offs2, out):
@@ -36,7 +37,7 @@ def tile_attend_wordmax_kernel(tc, query, keys_words, keys_scales, size, vals, o
         token_list = keep.tile([P, I // 16], U16, name="token_list")
         nc.sync.dma_start(token_list[:], offs)
         q_raw = shared("slot_s", [P, PACK, Q], F32, "q_raw")
-        nc.sync.dma_start(q_raw[:], query.rearrange("(p j) q -> p j q", j=PACK))
+        nc.scalar.dma_start(q_raw[:], query.rearrange("(p j) q -> p j q", j=PACK))
         word_list = keep.tile([P, G // 16], U16, name="word_list")
         nc.sync.dma_start(word_list[:], offs2)
         scale_pool = shared("slot_c", [P, T], U8, "scale_pool")
@@ -82,15 +83,11 @@ def tile_attend_wordmax_kernel(tc, query, keys_words, keys_scales, size, vals, o
 
         for b in range(3):
             load_values(b)
-        v_turned = keep.tile([P, E * PACK], BF16, name="v_turned", align_bytes=64)
 
-        def turn_values(b, picked):
+        def turn(bank, picked):
             pairs = picked[:].bitcast(F32)
-            bank = psum.tile([P, 2, P], F32, name="v_bank", tag="v_bank", bufs=2)
             for u in range(2):
                 nc.tensor.transpose(bank[:, u, :], pairs[:, u : G // 2 : 2], ident[:])
-            turned = v_turned[:, b * P * PACK : (b + 1) * P * PACK]
-            nc.scalar.copy(turned.bitcast(F32).rearrange("p (e u) -> p e u", u=2), bank[:].rearrange("p u e -> p e u"))
 
         def gather_on_scalar(b):
             window = shared("slot_w", [P, U], BF16, "v_window%d" % b)
@@ -99,26 +96,29 @@ def tile_attend_wordmax_kernel(tc, query, keys_words, keys_scales, size, vals, o
                 nc.scalar.activation(window[:, cols], v_raw[b][:, cols], ACT.Copy)
             picked = keep.tile([P, G], BF16, name="v_picked%d" % b, align_bytes=64)
             nc.scalar.activation(picked[:], window[:].indirect(word_list[:]), ACT.Copy)
-            turn_values(b, picked)
+            return picked
 
         def gather_on_vector(b):
             picked = keep.tile([P, G], BF16, name="v_picked%d" % b, align_bytes=64)
             nc.vector.tensor_copy(picked[:], v_raw[b][:].indirect(word_list[:]))
-            turn_values(b, picked)
+            return picked
 
-        s = keep.tile([P, G], F32, name="s")
+        s = shared("slot_e", [P, G], F32, "s")
         banks = []
 
-        def score(c):
-            key_codes = shared("slot_d" if c == 0 else "key_codes%d" % c, [P, CHUNK], U32, "key_codes%d" % c)
-            slots = token_list[:, c * CHUNK // 16 : (c + 1) * CHUNK // 16]
-            nc.vector.tensor_copy(key_codes[:], word_pool[:].bitcast(U32).indirect(slots))
+        def gather_keys(h):
+            half = shared("slot_d" if h == 0 else "key_codes1", [P, I // 2], U32, "key_codes%d" % h)
+            slots = token_list[:, h * I // 32 : (h + 1) * I // 32]
+            nc.vector.tensor_copy(half[:], word_pool[:].bitcast(U32).indirect(slots))
+            return half
+
+        def score(c, key_codes):
             bank = psum.tile([P, CHUNK], F32, name="acc", tag="acc", bufs=4)
             nc.tensor.matmul_mx(
                 out=bank[:],
                 lhsT=q_codes[:].bitcast(FP8X4),
                 lhsT_scale=q_scales[:],
-                rhs=key_codes[:].bitcast(FP8X4),
+                rhs=key_codes.bitcast(FP8X4),
                 rhs_scale=key_scales[:, c * CHUNK : (c + 1) * CHUNK],
                 start=True,
                 stop=True,
@@ -129,24 +129,30 @@ def tile_attend_wordmax_kernel(tc, query, keys_words, keys_scales, size, vals, o
             words = slice(c * CHUNK // PACK, (c + 1) * CHUNK // PACK)
             nc.vector.tensor_reduce(s[:, words], banks[c][:].rearrange("q (g r) -> q g r", r=PACK), AXIS_X, ALU.max)
 
-        gather_on_scalar(0)
-        gather_on_scalar(1)
-        chunks = I // CHUNK
-        for c in range(chunks):
-            score(c)
-            if c > 0:
-                best_token(c - 1)
-            else:
+        early_bank = psum.tile([P, 2, 2, P], F32, name="early_bank")
+        for b in range(2):
+            turn(early_bank[:, b], gather_on_scalar(b))
+        for h in range(2):
+            half = gather_keys(h)
+            for k in range(2):
+                score(2 * h + k, half[:, k * CHUNK : (k + 1) * CHUNK])
+            if h == 0:
                 load_values(3)
-        best_token(chunks - 1)
+        for c in range(I // CHUNK):
+            best_token(c)
 
         neg_max = keep.tile([P, 1], F32, name="neg_max")
         nc.vector.tensor_reduce(neg_max[:], s[:], AXIS_X, ALU.max, negate=True)
         p = shared("slot_w", [P, G], F32, "p")
         row_sum = keep.tile([P, 1], F32, name="row_sum")
         nc.scalar.activation(p[:], s[:], ACT.Exp, bias=neg_max[:], scale=1.0, accum_out=row_sum[:])
-        gather_on_vector(2)
-        gather_on_vector(3)
+        v_turned = shared("slot_e", [P, E * PACK], BF16, "v_turned")
+        v_pairs = v_turned[:].bitcast(F32).rearrange("p (b e u) -> p b e u", u=2, e=P)
+        nc.scalar.copy(v_pairs[:, 0:2], early_bank[:].rearrange("p b u e -> p b e u"))
+        for b in range(2, 4):
+            bank = psum.tile([P, 2, P], F32, name="acc", tag="acc", bufs=4)
+            turn(bank, gather_on_vector(b))
+            nc.scalar.copy(v_pairs[:, b], bank[:].rearrange("p u e -> p e u"))
         inv_sum = shared("slot_d", [P, 1], F32, "inv_sum")
         nc.vector.reciprocal(inv_sum[:], row_sum[:])
         w_bank = psum.tile([P, 2, P], F32, name="w_bank")
@@ -161,11 +167,9 @@ def tile_attend_wordmax_kernel(tc, query, keys_words, keys_scales, size, vals, o
                 ALU.mult,
             )
             nc.tensor.transpose(w_bank[:, u, :], w[:].rearrange("q p t -> q (p t)").bitcast(F32), ident[:])
+
         v_codes = shared("slot_w", [P, E], U32, "v_codes")
-        for lo, hi in ((0, 256), (256, 384), (384, 512)):
-            nc.vector.quantize_mx(
-                out=v_codes[:, lo:hi].bitcast(FP8X4), scales=v_scales[:, lo:hi], in_=v_turned[:, lo * PACK : hi * PACK]
-            )
+        nc.vector.quantize_mx(out=v_codes[:].bitcast(FP8X4), scales=v_scales[:], in_=v_turned[:])
         w_turned = keep.tile([P, Q * PACK], BF16, name="w_turned", align_bytes=64)
         nc.vector.tensor_copy(w_turned[:].bitcast(F32).rearrange("p (q u) -> p q u", u=2), w_bank[:].rearrange("p u q -> p q u"))
         w_codes = keep.tile([P, Q], U32, name="w_codes", align_bytes=64)
@@ -186,6 +190,7 @@ def tile_attend_wordmax_kernel(tc, query, keys_words, keys_scales, size, vals, o
             result = keep.tile([P, hi - lo], F32, name="result%d" % part)
             if part == len(PARTS) - 1:
                 nc.vector.tensor_copy(result[:], bank[:])
+                nc.sync.dma_start(out[:, lo:hi], result[:])
             else:
                 nc.scalar.copy(result[:], bank[:])
-            nc.sync.dma_start(out[:, lo:hi], result[:])
+                nc.scalar.dma_start(out[:, lo:hi], result[:])

@@ -19,8 +19,7 @@ AXIS_X = mybir.AxisListType.X
 
 P = 128
 PACK = 4
-CAST_PIECES = 4
-PIECE = U // CAST_PIECES
+PIECES = (4, 2, 1, 1)
 CHUNK = 512
 PARTS = ((0, 256), (256, 512))
 
@@ -75,7 +74,7 @@ def tile_attend_wordmax_kernel(tc, query, keys_words, keys_scales, size, vals, o
 
         def load_values(b):
             raw = shared(("slot_a", "slot_b", "slot_c", "slot_d")[b], [P, U], F32, "v_raw%d" % b)
-            pieces = CAST_PIECES if b < 2 else 1
+            pieces = PIECES[b]
             for h in range(pieces):
                 cols = slice(h * U // pieces, (h + 1) * U // pieces)
                 nc.sync.dma_start(raw[:, cols], vals[b * P : (b + 1) * P, cols])
@@ -85,25 +84,28 @@ def tile_attend_wordmax_kernel(tc, query, keys_words, keys_scales, size, vals, o
             load_values(b)
 
         def turn(bank, picked):
-            pairs = picked[:].bitcast(F32)
+            pairs = picked.bitcast(F32)
             for u in range(2):
                 nc.tensor.transpose(bank[:, u, :], pairs[:, u : G // 2 : 2], ident[:])
 
-        def gather_on_scalar(b):
+        def cast_on_scalar(b):
             window = shared("slot_w", [P, U], BF16, "v_window%d" % b)
-            for h in range(CAST_PIECES):
-                cols = slice(h * U // CAST_PIECES, (h + 1) * U // CAST_PIECES)
+            for h in range(PIECES[b]):
+                cols = slice(h * U // PIECES[b], (h + 1) * U // PIECES[b])
                 nc.scalar.activation(window[:, cols], v_raw[b][:, cols], ACT.Copy)
-            picked = keep.tile([P, G], BF16, name="v_picked%d" % b, align_bytes=64)
-            nc.scalar.activation(picked[:], window[:].indirect(word_list[:]), ACT.Copy)
-            return picked
+            return window
+
+        def gather_on_scalar(picked, window, lo, hi):
+            nc.scalar.activation(picked[:, lo:hi], window[:].indirect(word_list[:, lo // 16 : hi // 16]), ACT.Copy)
 
         def gather_on_vector(b):
             picked = keep.tile([P, G], BF16, name="v_picked%d" % b, align_bytes=64)
             nc.vector.tensor_copy(picked[:], v_raw[b][:].indirect(word_list[:]))
-            return picked
+            return picked[:]
 
-        s = shared("slot_e", [P, G], F32, "s")
+        overlay = keep.tile([P, G // 4 + G], F32, name="overlay", align_bytes=64)
+        s = overlay[:, G // 4 : G // 4 + G]
+        picked1 = overlay[:, 0 : G // 2].bitcast(BF16)
         banks = []
 
         def gather_keys(h):
@@ -129,9 +131,12 @@ def tile_attend_wordmax_kernel(tc, query, keys_words, keys_scales, size, vals, o
             words = slice(c * CHUNK // PACK, (c + 1) * CHUNK // PACK)
             nc.vector.tensor_reduce(s[:, words], banks[c][:].rearrange("q (g r) -> q g r", r=PACK), AXIS_X, ALU.max)
 
-        early_bank = psum.tile([P, 2, 2, P], F32, name="early_bank")
-        for b in range(2):
-            turn(early_bank[:, b], gather_on_scalar(b))
+        early_bank = psum.tile([P, 1, 2, P], F32, name="early_bank")
+        picked0 = keep.tile([P, G], BF16, name="v_picked0", align_bytes=64)
+        gather_on_scalar(picked0, cast_on_scalar(0), 0, G)
+        turn(early_bank[:, 0], picked0[:])
+        window1 = cast_on_scalar(1)
+        gather_on_scalar(picked1, window1, 0, G // 2)
         for h in range(2):
             half = gather_keys(h)
             for k in range(2):
@@ -141,17 +146,18 @@ def tile_attend_wordmax_kernel(tc, query, keys_words, keys_scales, size, vals, o
         for c in range(I // CHUNK):
             best_token(c)
 
-        neg_max = keep.tile([P, 1], F32, name="neg_max")
-        nc.vector.tensor_reduce(neg_max[:], s[:], AXIS_X, ALU.max, negate=True)
-        p = shared("slot_w", [P, G], F32, "p")
+        neg_max = shared("slot_e", [P, 1], F32, "neg_max")
+        nc.vector.tensor_reduce(neg_max[:], s, AXIS_X, ALU.max, negate=True)
+        p = shared("slot_b", [P, G], F32, "p")
         row_sum = keep.tile([P, 1], F32, name="row_sum")
-        nc.scalar.activation(p[:], s[:], ACT.Exp, bias=neg_max[:], scale=1.0, accum_out=row_sum[:])
+        nc.scalar.activation(p[:], s, ACT.Exp, bias=neg_max[:], scale=1.0, accum_out=row_sum[:])
+        gather_on_scalar(picked1, window1, G // 2, G)
         v_turned = shared("slot_e", [P, E * PACK], BF16, "v_turned")
         v_pairs = v_turned[:].bitcast(F32).rearrange("p (b e u) -> p b e u", u=2, e=P)
-        nc.scalar.copy(v_pairs[:, 0:2], early_bank[:].rearrange("p b u e -> p b e u"))
-        for b in range(2, 4):
+        nc.scalar.copy(v_pairs[:, 0], early_bank[:, 0].rearrange("p u e -> p e u"))
+        for b in (2, 1, 3):
             bank = psum.tile([P, 2, P], F32, name="acc", tag="acc", bufs=4)
-            turn(bank, gather_on_vector(b))
+            turn(bank, picked1 if b == 1 else gather_on_vector(b))
             nc.scalar.copy(v_pairs[:, b], bank[:].rearrange("p u e -> p e u"))
         inv_sum = shared("slot_d", [P, 1], F32, "inv_sum")
         nc.vector.reciprocal(inv_sum[:], row_sum[:])
@@ -168,10 +174,10 @@ def tile_attend_wordmax_kernel(tc, query, keys_words, keys_scales, size, vals, o
             )
             nc.tensor.transpose(w_bank[:, u, :], w[:].rearrange("q p t -> q (p t)").bitcast(F32), ident[:])
 
-        v_codes = shared("slot_w", [P, E], U32, "v_codes")
+        v_codes = shared("slot_b", [P, E], U32, "v_codes")
         nc.vector.quantize_mx(out=v_codes[:].bitcast(FP8X4), scales=v_scales[:], in_=v_turned[:])
         w_turned = keep.tile([P, Q * PACK], BF16, name="w_turned", align_bytes=64)
-        nc.vector.tensor_copy(w_turned[:].bitcast(F32).rearrange("p (q u) -> p q u", u=2), w_bank[:].rearrange("p u q -> p q u"))
+        nc.scalar.copy(w_turned[:].bitcast(F32).rearrange("p (q u) -> p q u", u=2), w_bank[:].rearrange("p u q -> p q u"))
         w_codes = keep.tile([P, Q], U32, name="w_codes", align_bytes=64)
         w_scales = keep.tile([P, Q], U8, name="w_scales", align_bytes=64)
         nc.vector.quantize_mx(out=w_codes[:].bitcast(FP8X4), scales=w_scales[:], in_=w_turned[:])

from contextlib import ExitStack

import concourse.mybir as mybir
from concourse.masks import make_identity

D, T, I, G, U, Q, E = 512, 4096, 2048, 512, 2048, 128, 512
FLOPS = 2 * D * Q * I + 2 * G * Q * E

F32 = mybir.dt.float32
BF16 = mybir.dt.bfloat16
I32 = mybir.dt.int32
U32 = mybir.dt.uint32
U16 = mybir.dt.uint16
U8 = mybir.dt.uint8
FP8X4 = mybir.dt.float8_e4m3fn_x4
ACT = mybir.ActivationFunctionType
ALU = mybir.AluOpType
AXIS_X = mybir.AxisListType.X

P = 128
PACK = 4
PIECES = (4, 2, 1, 1)
CHUNK = 512
PARTS = ((0, 256), (256, 512))


def tile_attend_wordmax_kernel(tc, query, keys_words, keys_scales, size, vals, offs, offs2, out):
    nc = tc.nc
    with ExitStack() as ctx:
        keep = ctx.enter_context(tc.tile_pool(name="keep", bufs=1))
        psum = ctx.enter_context(tc.psum_pool(name="psum", bufs=1))

        def shared(slot, shape, dtype, name):
            return keep.tile(shape, dtype, name=name, tag=slot, align_bytes=64)

        token_list = keep.tile([P, I // 16], U16, name="token_list")
        nc.sync.dma_start(token_list[:], offs)
        q_raw = shared("slot_s", [P, PACK, Q], F32, "q_raw")
        nc.scalar.dma_start(q_raw[:], query.rearrange("(p j) q -> p j q", j=PACK))
        word_list = keep.tile([P, G // 16], U16, name="word_list")
        nc.sync.dma_start(word_list[:], offs2)
        scale_pool = shared("slot_c", [P, T], U8, "scale_pool")
        nc.vector.memset(scale_pool[:].bitcast(I32), 0)
        for r in range(4):
            nc.sync.dma_start(scale_pool[r:P:32, :].bitcast(I32), keys_scales[0, r:16:4, :].bitcast(I32))

        ident = keep.tile([P, P], F32, name="ident")
        make_identity(nc, ident[:])
        zero = shared("slot_k", [P, 1], F32, "zero")
        nc.vector.memset(zero[:], 0.0)
        warm = shared("slot_a", [P, 1], F32, "warm")
        nc.scalar.activation(warm[:], zero[:], ACT.Exp)
        word_pool = shared("slot_k", [P, T], I32, "word_pool")
        nc.sync.dma_start(word_pool[:], keys_words[0].rearrange("p n t -> p (n t)").bitcast(I32))


        q_bf = shared("slot_b", [P, Q * PACK], BF16, "q_bf")
        nc.vector.tensor_copy(q_bf[:].rearrange("p (q j) -> p q j", j=PACK), q_raw[:].rearrange("p j q -> p q j"))
        q_codes = keep.tile([P, Q], U32, name="q_codes", align_bytes=64)
        q_scales = keep.tile([P, Q], U8, name="q_scales", align_bytes=64)
        nc.vector.quantize_mx(out=q_codes[:].bitcast(FP8X4), scales=q_scales[:], in_=q_bf[:])

        size_cols = shared("slot_s", [P, PACK], F32, "size_cols")
        nc.sync.dma_start(size_cols[:], size.rearrange("o (p t) -> p (o t)", t=PACK))
        size_bank = psum.tile([P, PACK, P], F32, name="size_bank")
        for t in range(PACK):
            nc.tensor.transpose(size_bank[:, t, :], size_cols[:, t : t + 1].to_broadcast([P, P]), ident[:])

        key_scales = keep.tile([P, I], U8, name="key_scales", align_bytes=64)
        nc.vector.tensor_copy(key_scales[:], scale_pool[:].indirect(token_list[:]))

        v_scales = keep.tile([P, E], U8, name="v_scales", align_bytes=64)
        v_raw = []

        def load_values(b):
            raw = shared(("slot_a", "slot_b", "slot_c", "slot_d")[b], [P, U], F32, "v_raw%d" % b)
            pieces = PIECES[b]
            for h in range(pieces):
                cols = slice(h * U // pieces, (h + 1) * U // pieces)
                nc.sync.dma_start(raw[:, cols], vals[b * P : (b + 1) * P, cols])
            v_raw.append(raw)

        for b in range(3):
            load_values(b)

        def turn(bank, picked):
            pairs = picked.bitcast(F32)
            for u in range(2):
                nc.tensor.transpose(bank[:, u, :], pairs[:, u : G // 2 : 2], ident[:])

        def cast_on_scalar(b):
            window = shared("slot_w", [P, U], BF16, "v_window%d" % b)
            for h in range(PIECES[b]):
                cols = slice(h * U // PIECES[b], (h + 1) * U // PIECES[b])
                nc.scalar.activation(window[:, cols], v_raw[b][:, cols], ACT.Copy)
            return window

        def gather_on_scalar(picked, window, lo, hi):
            nc.scalar.activation(picked[:, lo:hi], window[:].indirect(word_list[:, lo // 16 : hi // 16]), ACT.Copy)

        def gather_on_vector(b):
            picked = keep.tile([P, G], BF16, name="v_picked%d" % b, align_bytes=64)
            nc.vector.tensor_copy(picked[:], v_raw[b][:].indirect(word_list[:]))
            return picked[:]

        overlay = keep.tile([P, G // 4 + G], F32, name="overlay", align_bytes=64)
        s = overlay[:, G // 4 : G // 4 + G]
        picked1 = overlay[:, 0 : G // 2].bitcast(BF16)
        banks = []

        def gather_keys(h):
            half = shared("slot_d" if h == 0 else "key_codes1", [P, I // 2], U32, "key_codes%d" % h)
            slots = token_list[:, h * I // 32 : (h + 1) * I // 32]
            nc.vector.tensor_copy(half[:], word_pool[:].bitcast(U32).indirect(slots))
            return half

        def score(c, key_codes):
            bank = psum.tile([P, CHUNK], F32, name="acc", tag="acc", bufs=4)
            nc.tensor.matmul_mx(
                out=bank[:],
                lhsT=q_codes[:].bitcast(FP8X4),
                lhsT_scale=q_scales[:],
                rhs=key_codes.bitcast(FP8X4),
                rhs_scale=key_scales[:, c * CHUNK : (c + 1) * CHUNK],
                start=True,
                stop=True,
            )
            banks.append(bank)

        def best_token(c):
            words = slice(c * CHUNK // PACK, (c + 1) * CHUNK // PACK)
            nc.vector.tensor_reduce(s[:, words], banks[c][:].rearrange("q (g r) -> q g r", r=PACK), AXIS_X, ALU.max)

        early_bank = psum.tile([P, 1, 2, P], F32, name="early_bank")
        picked0 = keep.tile([P, G], BF16, name="v_picked0", align_bytes=64)
        gather_on_scalar(picked0, cast_on_scalar(0), 0, G)
        turn(early_bank[:, 0], picked0[:])
        window1 = cast_on_scalar(1)
        gather_on_scalar(picked1, window1, 0, G // 2)
        for h in range(2):
            half = gather_keys(h)
            for k in range(2):
                score(2 * h + k, half[:, k * CHUNK : (k + 1) * CHUNK])
            if h == 0:
                load_values(3)
        for c in range(I // CHUNK):
            best_token(c)

        neg_max = shared("slot_e", [P, 1], F32, "neg_max")
        nc.vector.tensor_reduce(neg_max[:], s, AXIS_X, ALU.max, negate=True)
        p = shared("slot_b", [P, G], F32, "p")
        row_sum = keep.tile([P, 1], F32, name="row_sum")
        nc.scalar.activation(p[:], s, ACT.Exp, bias=neg_max[:], scale=1.0, accum_out=row_sum[:])
        gather_on_scalar(picked1, window1, G // 2, G)
        v_turned = shared("slot_e", [P, E * PACK], BF16, "v_turned")
        v_pairs = v_turned[:].bitcast(F32).rearrange("p (b e u) -> p b e u", u=2, e=P)
        nc.scalar.copy(v_pairs[:, 0], early_bank[:, 0].rearrange("p u e -> p e u"))
        for b in (2, 1, 3):
            bank = psum.tile([P, 2, P], F32, name="acc", tag="acc", bufs=4)
            turn(bank, picked1 if b == 1 else gather_on_vector(b))
            nc.scalar.copy(v_pairs[:, b], bank[:].rearrange("p u e -> p e u"))
        inv_sum = shared("slot_d", [P, 1], F32, "inv_sum")
        nc.vector.reciprocal(inv_sum[:], row_sum[:])
        w_bank = psum.tile([P, 2, P], F32, name="w_bank")
        for u in range(2):
            w = keep.tile([P, P, 2], BF16, name="w%d" % u, align_bytes=64)
            nc.vector.scalar_tensor_tensor(
                w[:],
                p[:].rearrange("q (p t) -> q p t", t=PACK)[:, :, 2 * u : 2 * u + 2],
                inv_sum[:],
                size_bank[:, 2 * u : 2 * u + 2, :].rearrange("q t p -> q p t"),
                ALU.mult,
                ALU.mult,
            )
            nc.tensor.transpose(w_bank[:, u, :], w[:].rearrange("q p t -> q (p t)").bitcast(F32), ident[:])

        v_codes = shared("slot_b", [P, E], U32, "v_codes")
        nc.vector.quantize_mx(out=v_codes[:].bitcast(FP8X4), scales=v_scales[:], in_=v_turned[:])
        w_turned = keep.tile([P, Q * PACK], BF16, name="w_turned", align_bytes=64)
        nc.scalar.copy(w_turned[:].bitcast(F32).rearrange("p (q u) -> p q u", u=2), w_bank[:].rearrange("p u q -> p q u"))
        w_codes = keep.tile([P, Q], U32, name="w_codes", align_bytes=64)
        w_scales = keep.tile([P, Q], U8, name="w_scales", align_bytes=64)
        nc.vector.quantize_mx(out=w_codes[:].bitcast(FP8X4), scales=w_scales[:], in_=w_turned[:])

        for part, (lo, hi) in enumerate(PARTS):
            bank = psum.tile([P, hi - lo], F32, name="acc", tag="acc", bufs=4)
            nc.tensor.matmul_mx(
                out=bank[:],
                lhsT=w_codes[:].bitcast(FP8X4),
                lhsT_scale=w_scales[:],
                rhs=v_codes[:, lo:hi].bitcast(FP8X4),
                rhs_scale=v_scales[:, lo:hi],
                start=True,
                stop=True,
            )
            result = keep.tile([P, hi - lo], F32, name="result%d" % part)
            if part == len(PARTS) - 1:
                nc.vector.tensor_copy(result[:], bank[:])
                nc.sync.dma_start(out[:, lo:hi], result[:])
            else:
                nc.scalar.copy(result[:], bank[:])
                nc.scalar.dma_start(out[:, lo:hi], result[:])
